import numpy as np
import ml_dtypes


def mxq(x, axis, fmt="e4m3"):
    dtype, down = {"e4m3": (ml_dtypes.float8_e4m3fn, 7), "e5m2": (ml_dtypes.float8_e5m2, 14)}[fmt]
    v = np.moveaxis(np.asarray(x, np.float32).astype(ml_dtypes.bfloat16).astype(np.float64), axis, -1)
    blocks = v.reshape(v.shape[:-1] + (-1, 32))
    amax = np.abs(blocks).max(-1, keepdims=True)
    byte = np.maximum(np.where(amax > 0, np.frexp(amax)[1] - 1 + 127, 0) - down, 1)
    scale = np.exp2(byte - 127.0)
    codes = (blocks / scale).astype(np.float32).astype(dtype).astype(np.float64)
    return np.moveaxis((codes * scale).reshape(v.shape), -1, axis)


WIDE = False


def mx_kscale(k):
    if not WIDE:
        return np.ones(k)
    levels = np.array([10, -10, 5, -5, 0])
    if k % 512:
        return np.exp2(np.random.permutation(np.resize(levels, k // 32))).repeat(32)
    a = np.empty((k // 512, 16))
    for p in range(k // 512):
        a[p, :8] = np.random.permutation(np.resize(levels, 8))
        for g in range(8):
            far = levels[np.abs(levels - a[p, g]) >= 10]
            a[p, g + 8] = far[np.random.randint(len(far))]
    return np.exp2(a.ravel()).repeat(32)


def f64(x):
    return np.asarray(x).astype(np.float64)


def striped(idx):
    return np.tile(idx.reshape(-1, 16).T, (8, 1)).astype(np.uint16)


def unstriped(offs):
    return offs[:16].T.reshape(-1).astype(np.int64)


def pack_weight(w):
    k, n = w.shape
    w = f64(np.asarray(w, np.float32).astype(ml_dtypes.bfloat16)).reshape(k // 32, 32, n)
    amax = np.abs(w).max(1)
    byte = np.clip(np.where(amax > 0, np.frexp(amax)[1] - 1 + 127 - 7, 1), 1, 254)
    scaled = (w * np.exp2(127.0 - byte)[:, None, :]).reshape(k, n).astype(np.float32)
    words = np.ascontiguousarray(scaled.reshape(k // 512, 128, 4, n).transpose(0, 1, 3, 2)).astype(ml_dtypes.float8_e4m3fn).view(np.uint8)
    return words, np.ascontiguousarray(byte.astype(np.uint8).reshape(k // 512, 16, n))


def unpack_weight(words, scales):
    g, p, n, _ = words.shape
    vals = np.ascontiguousarray(words).view(ml_dtypes.float8_e4m3fn).astype(np.float64) * np.repeat(np.exp2(scales.astype(np.float64) - 127.0), 8, axis=1)[..., None]
    return vals.transpose(0, 1, 3, 2).reshape(g * 512, n)


K, T, S, J = 1024, 1024, 512, 512
P = 2 ** 7


def setup_inputs():
    n = np.random.standard_normal
    s = mx_kscale(K)[:, None]
    packed_xT = pack_weight(n((K, T)) * s)
    return {
        "x_words": packed_xT[0],
        "x_scales": packed_xT[1],
        "hT": (n((K, J)) / np.sqrt(K) / s).astype(np.float32),
        "corr": (np.tile(0.5 * np.random.standard_normal(T), (P, 1))).astype(np.float32),
        "offs": striped(np.random.permutation(T)[:S]),
    }


def reference(x_words, x_scales, hT, corr, offs):
    hTq = mxq(f64(hT), 0, "e4m3")
    xq = unpack_weight(x_words, x_scales)[:, unstriped(offs)]
    y = (hTq.T @ xq) + f64(corr)[:1][:, unstriped(offs)]
    e = np.exp(y - y.max(axis=1, keepdims=True))
    return e / e.sum(axis=1, keepdims=True)

@@ -1,0 +1,145 @@
+from contextlib import ExitStack
+
+import concourse.mybir as mybir
+from concourse.masks import make_identity
+
+K, T, S, J = 1024, 1024, 512, 512
+FLOPS = 2 * K * S * J
+
+F32 = mybir.dt.float32
+BF16 = mybir.dt.bfloat16
+I32 = mybir.dt.int32
+U32 = mybir.dt.uint32
+U16 = mybir.dt.uint16
+U8 = mybir.dt.uint8
+FP8X4 = mybir.dt.float8_e4m3fn_x4
+ALU = mybir.AluOpType
+ACT = mybir.ActivationFunctionType
+
+P = 128
+PACK = 4
+K_PASS = P * PACK
+PASSES = K // K_PASS
+TILES = J // P
+
+
+def tile_picked_zsoft_softmax_p_kernel(tc, x_words, x_scales, hT, corr, offs, out):
+    nc = tc.nc
+    with ExitStack() as ctx:
+        keep = ctx.enter_context(tc.tile_pool(name="keep", bufs=1))
+        psum = ctx.enter_context(tc.psum_pool(name="psum", bufs=1))
+
+        offsets = keep.tile([P, S // 16], U16, name="offsets")
+
+        scale_table = keep.tile([P, T], U8, name="scale_table", align_bytes=64)
+        nc.vector.memset(scale_table[:].bitcast(I32), 0)
+
+
+        word_table = [keep.tile([P, T], I32, name="word_table%d" % o, align_bytes=64) for o in range(PASSES)]
+        h_raw = {}
+        for i in range(TILES):
+            for o in range(PASSES):
+                h_raw[i, o] = keep.tile([P, PACK, P], F32, name="h_raw%d_%d" % (i, o), align_bytes=64)
+        corr_table = keep.tile([P, T], F32, name="corr_table", align_bytes=64)
+        corr_row = keep.tile([P, T // P], F32, name="corr_row", align_bytes=64)
+        nc.scalar.dma_start(corr_row[:], corr[0].rearrange("(p e) -> p e", p=P))
+        identity = keep.tile([P, P], F32, name="identity", align_bytes=64)
+        make_identity(nc, identity[:])
+
+        def load_words(o):
+            nc.sync.dma_start(word_table[o][:], x_words[o].rearrange("p n t -> p (n t)").bitcast(I32))
+
+        def load_h(i, o):
+            rows = hT[o * K_PASS : (o + 1) * K_PASS, i * P : (i + 1) * P]
+            nc.sync.dma_start(h_raw[i, o][:], rows.rearrange("(p j) c -> p j c", j=PACK))
+
+        load_words(0)
+        nc.sync.dma_start(offsets[:], offs)
+        for q in range(4):
+            nc.sync.dma_start(
+                scale_table[32 * q : 32 * q + 4 * PASSES, :].bitcast(I32),
+                x_scales[:, 4 * q : 4 * q + 4, :].bitcast(I32),
+            )
+        load_words(1)
+        load_h(0, 0)
+        load_h(0, 1)
+        for i in range(1, TILES):
+            for o in range(PASSES):
+                load_h(i, o)
+
+        x_scale = keep.tile([P, S], U8, name="x_scale", align_bytes=64)
+        x_codes = {}
+        h_codes, h_scale, logits, banks = {}, {}, {}, {}
+
+        def quantise(i, o):
+            grouped = keep.tile([P, P, PACK], BF16, name="grouped%d_%d" % (i, o), tag="grouped%d_%d" % (i, o), align_bytes=64)
+            nc.scalar.copy(
+                grouped[:].rearrange("p (c n) j -> p c j n", n=4),
+                h_raw[i, o][:].rearrange("p j (c n) -> p c j n", n=4),
+            )
+            h_codes[i, o] = keep.tile([P, P], U32, name="h_codes%d_%d" % (i, o), align_bytes=64)
+            h_scale[i, o] = keep.tile([P, P], U8, name="h_scale%d_%d" % (i, o), align_bytes=64)
+            nc.vector.quantize_mx(
+                out=h_codes[i, o][:].bitcast(FP8X4),
+                scales=h_scale[i, o][:],
+                in_=grouped[:].rearrange("p c j -> p (c j)"),
+            )
+
+        def multiply(i, o):
+            if o == 0:
+                banks[i] = psum.tile([P, S], F32, name="bank%d" % i)
+            nc.tensor.matmul_mx(
+                out=banks[i][:],
+                lhsT=h_codes[i, o][:].bitcast(FP8X4),
+                lhsT_scale=h_scale[i, o][:],
+                rhs=x_codes[o][:].bitcast(FP8X4),
+                rhs_scale=x_scale[4 * o : P, :],
+                start=(o == 0),
+                stop=(o == PASSES - 1),
+            )
+
+        def softmax(i):
+            z = keep.tile([P, S], F32, name="z%d" % i, align_bytes=64)
+            nc.vector.tensor_tensor(z[:], banks[i][:], corr_picked[:], ALU.add)
+            neg_max = keep.tile([P, 1], F32, name="neg_max%d" % i)
+            nc.vector.tensor_reduce(neg_max[:], z[:], mybir.AxisListType.X, ALU.max, negate=True)
+            e = keep.tile([P, S], F32, name="e%d" % i, align_bytes=64)
+            total = keep.tile([P, 1], F32, name="total%d" % i)
+            nc.scalar.activation(e[:], z[:], ACT.Exp, bias=neg_max[:], scale=1.0, accum_out=total[:])
+            inverse = keep.tile([P, 1], F32, name="inverse%d" % i)
+            nc.vector.reciprocal(inverse[:], total[:])
+            result = keep.tile([P, S], F32, name="result%d" % i, align_bytes=64)
+            engine = nc.vector if i == TILES - 1 else nc.gpsimd
+            engine.tensor_scalar(result[:], e[:], inverse[:], 0.0, ALU.mult, ALU.add)
+            nc.sync.dma_start(out[i * P : (i + 1) * P, :], result[:])
+
+        warm_out = keep.tile([P, 1], F32, name="warm_out")
+        nc.scalar.activation(warm_out[:], identity[:, 0:1], ACT.Exp)
+        for b in range(2):
+            spread = psum.tile([P, 4, P], F32, name="spread%d" % b)
+            for e in range(4):
+                column = corr_row[:, 4 * b + e : 4 * b + e + 1]
+                nc.tensor.transpose(spread[:, e, :], column.to_broadcast([P, P]), identity[:])
+            nc.scalar.copy(
+                corr_table[:].rearrange("m (p e) -> m p e", p=P)[:, :, 4 * b : 4 * b + 4],
+                spread[:].rearrange("m e p -> m p e"),
+            )
+
+        def gather_words(o):
+            x_codes[o] = keep.tile([P, S], U32, name="x_codes%d" % o, align_bytes=64)
+            nc.vector.tensor_copy(x_codes[o][:], word_table[o][:].bitcast(U32).indirect(offsets[:]))
+
+        gather_words(0)
+        nc.vector.tensor_copy(x_scale[:], scale_table[:].indirect(offsets[:]))
+        gather_words(1)
+        for o in range(PASSES):
+            quantise(0, o)
+            multiply(0, o)
+        corr_picked = keep.tile([P, S], F32, name="corr_picked", tag="grouped0_1", align_bytes=64)
+        nc.vector.tensor_copy(corr_picked[:], corr_table[:].indirect(offsets[:]))
+        for i in range(1, TILES):
+            for o in range(PASSES):
+                quantise(i, o)
+                multiply(i, o)
+        for i in range(TILES):
+            softmax(i)

@@ -1,7 +1,6 @@
 from contextlib import ExitStack
 
 import concourse.mybir as mybir
-from concourse.masks import make_identity
 
 K, T, S, J = 1024, 1024, 512, 512
 FLOPS = 2 * K * S * J
@@ -17,10 +16,27 @@ ALU = mybir.AluOpType
 ACT = mybir.ActivationFunctionType
 
 P = 128
+QUAD = 32
 PACK = 4
 K_PASS = P * PACK
 PASSES = K // K_PASS
 TILES = J // P
+CHUNKS = ((0,), (1,), (2, 3))
+
+
+def build_identity(nc, keep):
+    ones = keep.tile([P, P], F32, name="ones", align_bytes=64)
+    nc.vector.memset(ones[:], 1.0)
+    quadrant_start = keep.tile([P, 1], F32, name="quadrant_start")
+    for q in range(P // QUAD):
+        nc.vector.memset(quadrant_start[QUAD * q : QUAD * (q + 1), :], float(QUAD * q))
+    column = keep.tile([P, P], F32, name="column", align_bytes=64)
+    nc.vector.tensor_tensor_scan(column[:], ones[:], ones[:], -1.0, ALU.mult, ALU.add)
+    within = keep.tile([P, QUAD], F32, name="within", align_bytes=64)
+    nc.vector.transpose(within[:], column[:, 0:QUAD])
+    identity = keep.tile([P, P], F32, name="identity", align_bytes=64)
+    nc.vector.tensor_scalar(identity[:], column[:], within[:, 0:1], quadrant_start[:], ALU.subtract, ALU.is_equal)
+    return identity, ones
 
 
 def tile_picked_zsoft_softmax_p_kernel(tc, x_words, x_scales, hT, corr, offs, out):
@@ -29,53 +45,54 @@ def tile_picked_zsoft_softmax_p_kernel(tc, x_words, x_scales, hT, corr, offs, ou
         keep = ctx.enter_context(tc.tile_pool(name="keep", bufs=1))
         psum = ctx.enter_context(tc.psum_pool(name="psum", bufs=1))
 
-        offsets = keep.tile([P, S // 16], U16, name="offsets")
-
         scale_table = keep.tile([P, T], U8, name="scale_table", align_bytes=64)
         nc.vector.memset(scale_table[:].bitcast(I32), 0)
+        identity, ones = build_identity(nc, keep)
+        warm = keep.tile([P, 1], F32, name="warm")
+        nc.scalar.activation(warm[:], ones[:, 0:1], ACT.Exp)
 
-
-        word_table = [keep.tile([P, T], I32, name="word_table%d" % o, align_bytes=64) for o in range(PASSES)]
-        h_raw = {}
-        for i in range(TILES):
-            for o in range(PASSES):
-                h_raw[i, o] = keep.tile([P, PACK, P], F32, name="h_raw%d_%d" % (i, o), align_bytes=64)
-        corr_table = keep.tile([P, T], F32, name="corr_table", align_bytes=64)
-        corr_row = keep.tile([P, T // P], F32, name="corr_row", align_bytes=64)
-        nc.scalar.dma_start(corr_row[:], corr[0].rearrange("(p e) -> p e", p=P))
-        identity = keep.tile([P, P], F32, name="identity", align_bytes=64)
-        make_identity(nc, identity[:])
+        word_table, h_raw = {}, {}
 
         def load_words(o):
+            word_table[o] = keep.tile([P, T], I32, name="word_table%d" % o, align_bytes=64)
             nc.sync.dma_start(word_table[o][:], x_words[o].rearrange("p n t -> p (n t)").bitcast(I32))
 
-        def load_h(i, o):
-            rows = hT[o * K_PASS : (o + 1) * K_PASS, i * P : (i + 1) * P]
-            nc.sync.dma_start(h_raw[i, o][:], rows.rearrange("(p j) c -> p j c", j=PACK))
+        def load_h(c, o):
+            tiles = CHUNKS[c]
+            raw = keep.tile([P, PACK, P * len(tiles)], F32, name="h_raw", tag="h_raw%d_%d" % (c, o), align_bytes=64)
+            rows = hT[o * K_PASS : (o + 1) * K_PASS, tiles[0] * P : (tiles[-1] + 1) * P]
+            nc.sync.dma_start(raw[:], rows.rearrange("(p j) c -> p j c", j=PACK))
+            for n, i in enumerate(tiles):
+                h_raw[i, o] = raw[:, :, n * P : (n + 1) * P]
 
+        corr_row = keep.tile([P, T // P], F32, name="corr_row", align_bytes=64)
+        nc.sync.dma_start(corr_row[:], corr[0].rearrange("(p e) -> p e", p=P))
         load_words(0)
+        offsets = keep.tile([P, S // 16], U16, name="offsets")
         nc.sync.dma_start(offsets[:], offs)
         for q in range(4):
             nc.sync.dma_start(
                 scale_table[32 * q : 32 * q + 4 * PASSES, :].bitcast(I32),
                 x_scales[:, 4 * q : 4 * q + 4, :].bitcast(I32),
             )
-        load_words(1)
         load_h(0, 0)
+        load_words(1)
         load_h(0, 1)
-        for i in range(1, TILES):
+        for c in range(1, len(CHUNKS)):
             for o in range(PASSES):
-                load_h(i, o)
+                load_h(c, o)
 
-        x_scale = keep.tile([P, S], U8, name="x_scale", align_bytes=64)
-        x_codes = {}
-        h_codes, h_scale, logits, banks = {}, {}, {}, {}
+        x_codes, h_codes, h_scale, banks, logits, exps = {}, {}, {}, {}, {}, {}
+
+        def gather_words(o, tag):
+            x_codes[o] = keep.tile([P, S], U32, name="x_codes", tag=tag, align_bytes=64)
+            nc.vector.tensor_copy(x_codes[o][:], word_table[o][:].bitcast(U32).indirect(offsets[:]))
 
         def quantise(i, o):
-            grouped = keep.tile([P, P, PACK], BF16, name="grouped%d_%d" % (i, o), tag="grouped%d_%d" % (i, o), align_bytes=64)
+            grouped = keep.tile([P, P, PACK], BF16, name="grouped%d_%d" % (i, o), align_bytes=64)
             nc.scalar.copy(
                 grouped[:].rearrange("p (c n) j -> p c j n", n=4),
-                h_raw[i, o][:].rearrange("p j (c n) -> p c j n", n=4),
+                h_raw[i, o].rearrange("p j (c n) -> p c j n", n=4),
             )
             h_codes[i, o] = keep.tile([P, P], U32, name="h_codes%d_%d" % (i, o), align_bytes=64)
             h_scale[i, o] = keep.tile([P, P], U8, name="h_scale%d_%d" % (i, o), align_bytes=64)
@@ -98,23 +115,42 @@ def tile_picked_zsoft_softmax_p_kernel(tc, x_words, x_scales, hT, corr, offs, ou
                 stop=(o == PASSES - 1),
             )
 
-        def softmax(i):
-            z = keep.tile([P, S], F32, name="z%d" % i, align_bytes=64)
-            nc.vector.tensor_tensor(z[:], banks[i][:], corr_picked[:], ALU.add)
-            neg_max = keep.tile([P, 1], F32, name="neg_max%d" % i)
-            nc.vector.tensor_reduce(neg_max[:], z[:], mybir.AxisListType.X, ALU.max, negate=True)
+        def add_correction(i):
+            tag = {0: "h_raw1_1", 1: "h_raw2_1"}.get(i, "logits%d" % i)
+            logits[i] = keep.tile([P, S], F32, name="logits", tag=tag, align_bytes=64)
+            nc.vector.tensor_tensor(logits[i][:], banks[i][:], corr_picked[:], ALU.add)
+
+        def exponentiate(i):
+            tag = "h_raw2_0" if i < 2 else "neg_max%d" % i
+            neg_max = keep.tile([P, 1], F32, name="neg_max", tag=tag, align_bytes=64)
+            nc.vector.tensor_reduce(neg_max[:], logits[i][:], mybir.AxisListType.X, ALU.max, negate=True)
             e = keep.tile([P, S], F32, name="e%d" % i, align_bytes=64)
             total = keep.tile([P, 1], F32, name="total%d" % i)
-            nc.scalar.activation(e[:], z[:], ACT.Exp, bias=neg_max[:], scale=1.0, accum_out=total[:])
+            nc.scalar.activation(e[:], logits[i][:], ACT.Exp, bias=neg_max[:], scale=1.0, accum_out=total[:])
+            exps[i] = (e, total)
+
+        def normalise(i):
+            e, total = exps[i]
             inverse = keep.tile([P, 1], F32, name="inverse%d" % i)
             nc.vector.reciprocal(inverse[:], total[:])
-            result = keep.tile([P, S], F32, name="result%d" % i, align_bytes=64)
-            engine = nc.vector if i == TILES - 1 else nc.gpsimd
-            engine.tensor_scalar(result[:], e[:], inverse[:], 0.0, ALU.mult, ALU.add)
-            nc.sync.dma_start(out[i * P : (i + 1) * P, :], result[:])
+            rows = slice(i * P, (i + 1) * P)
+            if i < TILES - 1:
+                result = keep.tile([P, S], F32, name="result%d" % i, align_bytes=64)
+                if i < 2:
+                    nc.scalar.activation(result[:], e[:], ACT.Copy, scale=inverse[:])
+                else:
+                    nc.vector.tensor_scalar(result[:], e[:], inverse[:], None, ALU.mult)
+                nc.sync.dma_start(out[rows, :], result[:])
+            else:
+                split = 320
+                left = keep.tile([P, split], F32, name="left", align_bytes=64)
+                right = keep.tile([P, S - split], F32, name="right", align_bytes=64)
+                nc.vector.tensor_scalar(left[:], e[:, :split], inverse[:], None, ALU.mult)
+                nc.sync.dma_start(out[rows, :split], left[:])
+                nc.scalar.activation(right[:], e[:, split:], ACT.Copy, scale=inverse[:])
+                nc.scalar.dma_start(out[rows, split:], right[:])
 
-        warm_out = keep.tile([P, 1], F32, name="warm_out")
-        nc.scalar.activation(warm_out[:], identity[:, 0:1], ACT.Exp)
+        corr_table = keep.tile([P, T], F32, name="corr_table", align_bytes=64)
         for b in range(2):
             spread = psum.tile([P, 4, P], F32, name="spread%d" % b)
             for e in range(4):
@@ -125,21 +161,25 @@ def tile_picked_zsoft_softmax_p_kernel(tc, x_words, x_scales, hT, corr, offs, ou
                 spread[:].rearrange("m e p -> m p e"),
             )
 
-        def gather_words(o):
-            x_codes[o] = keep.tile([P, S], U32, name="x_codes%d" % o, align_bytes=64)
-            nc.vector.tensor_copy(x_codes[o][:], word_table[o][:].bitcast(U32).indirect(offsets[:]))
-
-        gather_words(0)
+        gather_words(0, "x_codes0")
+        x_scale = keep.tile([P, S], U8, name="x_scale", align_bytes=64)
         nc.vector.tensor_copy(x_scale[:], scale_table[:].indirect(offsets[:]))
-        gather_words(1)
-        for o in range(PASSES):
-            quantise(0, o)
-            multiply(0, o)
-        corr_picked = keep.tile([P, S], F32, name="corr_picked", tag="grouped0_1", align_bytes=64)
+        quantise(0, 0)
+        multiply(0, 0)
+        gather_words(1, "h_raw0_0")
+        quantise(0, 1)
+        multiply(0, 1)
+        corr_picked = keep.tile([P, S], F32, name="corr_picked", tag="h_raw0_1", align_bytes=64)
         nc.vector.tensor_copy(corr_picked[:], corr_table[:].indirect(offsets[:]))
-        for i in range(1, TILES):
+        for tiles in CHUNKS[1:]:
             for o in range(PASSES):
-                quantise(i, o)
-                multiply(i, o)
+                for i in tiles:
+                    quantise(i, o)
+                    multiply(i, o)
         for i in range(TILES):
-            softmax(i)
+            add_correction(i)
+            if 1 <= i <= 2:
+                normalise(i - 1)
+            exponentiate(i)
+        normalise(TILES - 2)
+        normalise(TILES - 1)

@@ -21,7 +21,7 @@ PACK = 4
 K_PASS = P * PACK
 PASSES = K // K_PASS
 TILES = J // P
-CHUNKS = ((0,), (1,), (2, 3))
+CHUNKS = ((0,), (1,), (2,), (3,))
 
 
 def build_identity(nc, keep):
@@ -116,13 +116,12 @@ def tile_picked_zsoft_softmax_p_kernel(tc, x_words, x_scales, hT, corr, offs, ou
             )
 
         def add_correction(i):
-            tag = {0: "h_raw1_1", 1: "h_raw2_1"}.get(i, "logits%d" % i)
+            tag = "h_raw%d_1" % (i + 1)
             logits[i] = keep.tile([P, S], F32, name="logits", tag=tag, align_bytes=64)
             nc.vector.tensor_tensor(logits[i][:], banks[i][:], corr_picked[:], ALU.add)
 
         def exponentiate(i):
-            tag = "h_raw2_0" if i < 2 else "neg_max%d" % i
-            neg_max = keep.tile([P, 1], F32, name="neg_max", tag=tag, align_bytes=64)
+            neg_max = keep.tile([P, 1], F32, name="neg_max%d" % i)
             nc.vector.tensor_reduce(neg_max[:], logits[i][:], mybir.AxisListType.X, ALU.max, negate=True)
             e = keep.tile([P, S], F32, name="e%d" % i, align_bytes=64)
             total = keep.tile([P, 1], F32, name="total%d" % i)
@@ -171,15 +170,20 @@ def tile_picked_zsoft_softmax_p_kernel(tc, x_words, x_scales, hT, corr, offs, ou
         multiply(0, 1)
         corr_picked = keep.tile([P, S], F32, name="corr_picked", tag="h_raw0_1", align_bytes=64)
         nc.vector.tensor_copy(corr_picked[:], corr_table[:].indirect(offsets[:]))
-        for tiles in CHUNKS[1:]:
+        for i in range(1, TILES - 1):
             for o in range(PASSES):
-                for i in tiles:
-                    quantise(i, o)
-                    multiply(i, o)
+                quantise(i, o)
+                multiply(i, o)
         for i in range(TILES):
             add_correction(i)
-            if 1 <= i <= 2:
-                normalise(i - 1)
+            if i == 1:
+                for o in range(PASSES):
+                    quantise(TILES - 1, o)
+                    multiply(TILES - 1, o)
+            if i == 2:
+                normalise(1)
             exponentiate(i)
+            if i == 1:
+                normalise(0)
         normalise(TILES - 2)
         normalise(TILES - 1)

@@ -82,7 +82,7 @@ def tile_picked_zsoft_softmax_p_kernel(tc, x_words, x_scales, hT, corr, offs, ou
             for o in range(PASSES):
                 load_h(c, o)
 
-        x_codes, h_codes, h_scale, banks, logits, exps = {}, {}, {}, {}, {}, {}
+        x_codes, h_codes, h_scale, banks, logits, neg_max, exps = {}, {}, {}, {}, {}, {}, {}
 
         def gather_words(o, tag):
             x_codes[o] = keep.tile([P, S], U32, name="x_codes", tag=tag, align_bytes=64)
@@ -116,16 +116,19 @@ def tile_picked_zsoft_softmax_p_kernel(tc, x_words, x_scales, hT, corr, offs, ou
             )
 
         def add_correction(i):
-            tag = "h_raw%d_1" % (i + 1)
+            tag = "h_raw%d_1" % (i + 1) if i < 2 else "logits%d" % i
             logits[i] = keep.tile([P, S], F32, name="logits", tag=tag, align_bytes=64)
             nc.vector.tensor_tensor(logits[i][:], banks[i][:], corr_picked[:], ALU.add)
 
+        def maximum(i):
+            neg_max[i] = keep.tile([P, 1], F32, name="neg_max%d" % i)
+            nc.vector.tensor_reduce(neg_max[i][:], logits[i][:], mybir.AxisListType.X, ALU.max, negate=True)
+
         def exponentiate(i):
-            neg_max = keep.tile([P, 1], F32, name="neg_max%d" % i)
-            nc.vector.tensor_reduce(neg_max[:], logits[i][:], mybir.AxisListType.X, ALU.max, negate=True)
-            e = keep.tile([P, S], F32, name="e%d" % i, align_bytes=64)
+            tag = "h_raw3_1" if i == 0 else "e%d" % i
+            e = keep.tile([P, S], F32, name="e", tag=tag, align_bytes=64)
             total = keep.tile([P, 1], F32, name="total%d" % i)
-            nc.scalar.activation(e[:], logits[i][:], ACT.Exp, bias=neg_max[:], scale=1.0, accum_out=total[:])
+            nc.scalar.activation(e[:], logits[i][:], ACT.Exp, bias=neg_max[i][:], scale=1.0, accum_out=total[:])
             exps[i] = (e, total)
 
         def normalise(i):
@@ -136,7 +139,7 @@ def tile_picked_zsoft_softmax_p_kernel(tc, x_words, x_scales, hT, corr, offs, ou
             if i < TILES - 1:
                 result = keep.tile([P, S], F32, name="result%d" % i, align_bytes=64)
                 if i < 2:
-                    nc.scalar.activation(result[:], e[:], ACT.Copy, scale=inverse[:])
+                    nc.gpsimd.tensor_scalar(result[:], e[:], inverse[:], 0.0, ALU.mult, ALU.add)
                 else:
                     nc.vector.tensor_scalar(result[:], e[:], inverse[:], None, ALU.mult)
                 nc.sync.dma_start(out[rows, :], result[:])
@@ -174,16 +177,20 @@ def tile_picked_zsoft_softmax_p_kernel(tc, x_words, x_scales, hT, corr, offs, ou
             for o in range(PASSES):
                 quantise(i, o)
                 multiply(i, o)
-        for i in range(TILES):
+        add_correction(0)
+        quantise_last = lambda o: (quantise(TILES - 1, o), multiply(TILES - 1, o))
+        maximum(0)
+        add_correction(1)
+        quantise_last(0)
+        maximum(1)
+        quantise_last(1)
+        exponentiate(0)
+        exponentiate(1)
+        for i in (2, 3):
             add_correction(i)
-            if i == 1:
-                for o in range(PASSES):
-                    quantise(TILES - 1, o)
-                    multiply(TILES - 1, o)
-            if i == 2:
-                normalise(1)
+            normalise(i - 2)
+        for i in (2, 3):
+            maximum(i)
             exponentiate(i)
-            if i == 1:
-                normalise(0)
-        normalise(TILES - 2)
-        normalise(TILES - 1)
+        for i in (2, 3):
+            normalise(i)

from contextlib import ExitStack

import concourse.mybir as mybir

K, T, S, J = 1024, 1024, 512, 512
FLOPS = 2 * K * S * J

F32 = mybir.dt.float32
BF16 = mybir.dt.bfloat16
I32 = mybir.dt.int32
U32 = mybir.dt.uint32
U16 = mybir.dt.uint16
U8 = mybir.dt.uint8
FP8X4 = mybir.dt.float8_e4m3fn_x4
ALU = mybir.AluOpType
ACT = mybir.ActivationFunctionType

P = 128
QUAD = 32
PACK = 4
K_PASS = P * PACK
PASSES = K // K_PASS
TILES = J // P
CHUNKS = ((0,), (1,), (2,), (3,))


def build_identity(nc, keep):
    ones = keep.tile([P, P], F32, name="ones", align_bytes=64)
    nc.vector.memset(ones[:], 1.0)
    quadrant_start = keep.tile([P, 1], F32, name="quadrant_start")
    for q in range(P // QUAD):
        nc.vector.memset(quadrant_start[QUAD * q : QUAD * (q + 1), :], float(QUAD * q))
    column = keep.tile([P, P], F32, name="column", align_bytes=64)
    nc.vector.tensor_tensor_scan(column[:], ones[:], ones[:], -1.0, ALU.mult, ALU.add)
    within = keep.tile([P, QUAD], F32, name="within", align_bytes=64)
    nc.vector.transpose(within[:], column[:, 0:QUAD])
    identity = keep.tile([P, P], F32, name="identity", align_bytes=64)
    nc.vector.tensor_scalar(identity[:], column[:], within[:, 0:1], quadrant_start[:], ALU.subtract, ALU.is_equal)
    return identity, ones


def tile_picked_zsoft_softmax_p_kernel(tc, x_words, x_scales, hT, corr, offs, out):
    nc = tc.nc
    with ExitStack() as ctx:
        keep = ctx.enter_context(tc.tile_pool(name="keep", bufs=1))
        psum = ctx.enter_context(tc.psum_pool(name="psum", bufs=1))

        scale_table = keep.tile([P, T], U8, name="scale_table", align_bytes=64)
        nc.vector.memset(scale_table[:].bitcast(I32), 0)
        identity, ones = build_identity(nc, keep)
        warm = keep.tile([P, 1], F32, name="warm")
        nc.scalar.activation(warm[:], ones[:, 0:1], ACT.Exp)

        word_table, h_raw = {}, {}

        def load_words(o):
            word_table[o] = keep.tile([P, T], I32, name="word_table%d" % o, align_bytes=64)
            nc.sync.dma_start(word_table[o][:], x_words[o].rearrange("p n t -> p (n t)").bitcast(I32))

        def load_h(c, o):
            tiles = CHUNKS[c]
            raw = keep.tile([P, PACK, P * len(tiles)], F32, name="h_raw", tag="h_raw%d_%d" % (c, o), align_bytes=64)
            rows = hT[o * K_PASS : (o + 1) * K_PASS, tiles[0] * P : (tiles[-1] + 1) * P]
            nc.sync.dma_start(raw[:], rows.rearrange("(p j) c -> p j c", j=PACK))
            for n, i in enumerate(tiles):
                h_raw[i, o] = raw[:, :, n * P : (n + 1) * P]

        corr_row = keep.tile([P, T // P], F32, name="corr_row", align_bytes=64)
        nc.sync.dma_start(corr_row[:], corr[0].rearrange("(p e) -> p e", p=P))
        load_words(0)
        offsets = keep.tile([P, S // 16], U16, name="offsets")
        nc.sync.dma_start(offsets[:], offs)
        for q in range(4):
            nc.sync.dma_start(
                scale_table[32 * q : 32 * q + 4 * PASSES, :].bitcast(I32),
                x_scales[:, 4 * q : 4 * q + 4, :].bitcast(I32),
            )
        load_h(0, 0)
        load_words(1)
        load_h(0, 1)
        for c in range(1, len(CHUNKS)):
            for o in range(PASSES):
                load_h(c, o)

        x_codes, h_codes, h_scale, banks, logits, neg_max, exps = {}, {}, {}, {}, {}, {}, {}

        def gather_words(o, tag):
            x_codes[o] = keep.tile([P, S], U32, name="x_codes", tag=tag, align_bytes=64)
            nc.vector.tensor_copy(x_codes[o][:], word_table[o][:].bitcast(U32).indirect(offsets[:]))

        def quantise(i, o):
            grouped = keep.tile([P, P, PACK], BF16, name="grouped%d_%d" % (i, o), align_bytes=64)
            nc.scalar.copy(
                grouped[:].rearrange("p (c n) j -> p c j n", n=4),
                h_raw[i, o].rearrange("p j (c n) -> p c j n", n=4),
            )
            h_codes[i, o] = keep.tile([P, P], U32, name="h_codes%d_%d" % (i, o), align_bytes=64)
            h_scale[i, o] = keep.tile([P, P], U8, name="h_scale%d_%d" % (i, o), align_bytes=64)
            nc.vector.quantize_mx(
                out=h_codes[i, o][:].bitcast(FP8X4),
                scales=h_scale[i, o][:],
                in_=grouped[:].rearrange("p c j -> p (c j)"),
            )

        def multiply(i, o):
            if o == 0:
                banks[i] = psum.tile([P, S], F32, name="bank%d" % i)
            nc.tensor.matmul_mx(
                out=banks[i][:],
                lhsT=h_codes[i, o][:].bitcast(FP8X4),
                lhsT_scale=h_scale[i, o][:],
                rhs=x_codes[o][:].bitcast(FP8X4),
                rhs_scale=x_scale[4 * o : P, :],
                start=(o == 0),
                stop=(o == PASSES - 1),
            )

        def add_correction(i):
            tag = "h_raw%d_1" % (i + 1) if i < 2 else "logits%d" % i
            logits[i] = keep.tile([P, S], F32, name="logits", tag=tag, align_bytes=64)
            nc.vector.tensor_tensor(logits[i][:], banks[i][:], corr_picked[:], ALU.add)

        def maximum(i):
            neg_max[i] = keep.tile([P, 1], F32, name="neg_max%d" % i)
            nc.vector.tensor_reduce(neg_max[i][:], logits[i][:], mybir.AxisListType.X, ALU.max, negate=True)

        def exponentiate(i):
            tag = "h_raw3_1" if i == 0 else "e%d" % i
            e = keep.tile([P, S], F32, name="e", tag=tag, align_bytes=64)
            total = keep.tile([P, 1], F32, name="total%d" % i)
            nc.scalar.activation(e[:], logits[i][:], ACT.Exp, bias=neg_max[i][:], scale=1.0, accum_out=total[:])
            exps[i] = (e, total)

        def normalise(i):
            e, total = exps[i]
            inverse = keep.tile([P, 1], F32, name="inverse%d" % i)
            nc.vector.reciprocal(inverse[:], total[:])
            rows = slice(i * P, (i + 1) * P)
            if i < TILES - 1:
                result = keep.tile([P, S], F32, name="result%d" % i, align_bytes=64)
                if i < 2:
                    nc.gpsimd.tensor_scalar(result[:], e[:], inverse[:], 0.0, ALU.mult, ALU.add)
                else:
                    nc.vector.tensor_scalar(result[:], e[:], inverse[:], None, ALU.mult)
                nc.sync.dma_start(out[rows, :], result[:])
            else:
                split = 320
                left = keep.tile([P, split], F32, name="left", align_bytes=64)
                right = keep.tile([P, S - split], F32, name="right", align_bytes=64)
                nc.vector.tensor_scalar(left[:], e[:, :split], inverse[:], None, ALU.mult)
                nc.sync.dma_start(out[rows, :split], left[:])
                nc.scalar.activation(right[:], e[:, split:], ACT.Copy, scale=inverse[:])
                nc.scalar.dma_start(out[rows, split:], right[:])

        corr_table = keep.tile([P, T], F32, name="corr_table", align_bytes=64)
        for b in range(2):
            spread = psum.tile([P, 4, P], F32, name="spread%d" % b)
            for e in range(4):
                column = corr_row[:, 4 * b + e : 4 * b + e + 1]
                nc.tensor.transpose(spread[:, e, :], column.to_broadcast([P, P]), identity[:])
            nc.scalar.copy(
                corr_table[:].rearrange("m (p e) -> m p e", p=P)[:, :, 4 * b : 4 * b + 4],
                spread[:].rearrange("m e p -> m p e"),
            )

        gather_words(0, "x_codes0")
        x_scale = keep.tile([P, S], U8, name="x_scale", align_bytes=64)
        nc.vector.tensor_copy(x_scale[:], scale_table[:].indirect(offsets[:]))
        quantise(0, 0)
        multiply(0, 0)
        gather_words(1, "h_raw0_0")
        quantise(0, 1)
        multiply(0, 1)
        corr_picked = keep.tile([P, S], F32, name="corr_picked", tag="h_raw0_1", align_bytes=64)
        nc.vector.tensor_copy(corr_picked[:], corr_table[:].indirect(offsets[:]))
        for i in range(1, TILES - 1):
            for o in range(PASSES):
                quantise(i, o)
                multiply(i, o)
        add_correction(0)
        quantise_last = lambda o: (quantise(TILES - 1, o), multiply(TILES - 1, o))
        maximum(0)
        add_correction(1)
        quantise_last(0)
        maximum(1)
        quantise_last(1)
        exponentiate(0)
        exponentiate(1)
        for i in (2, 3):
            add_correction(i)
            normalise(i - 2)
        for i in (2, 3):
            maximum(i)
            exponentiate(i)
        for i in (2, 3):
            normalise(i)
